import numpy as np
import ml_dtypes

BF16 = ml_dtypes.bfloat16


def bf(x):
    return np.asarray(x, np.float32).astype(BF16)


def f32(x):
    return np.asarray(x, np.float32)


def f64(x):
    return np.asarray(x).astype(np.float64)


def striped(idx):
    return np.tile(idx.reshape(-1, 16).T, (8, 1))


S, K, M, N, B, Q = 512, 512, 256, 256, 2, 128


def setup_inputs():
    return {"base": bf(np.random.standard_normal((B, M, S))), "x": bf(np.random.standard_normal((K, N))), "w": bf(np.random.standard_normal((K, M)) / np.sqrt(K)), "s": f32(0.5 + np.random.random_sample((M, 1))), "b": f32(0.5 * np.random.standard_normal((M, 1))), "offs": striped(np.random.permutation(S)[:N])}


def reference(base, x, w, s, b, offs):
    idx = offs[:16].T.reshape(-1)
    z = f64(base).copy()
    for i in range(B):
        z[i][:, idx[i * Q : (i + 1) * Q]] += f64(w).T @ f64(x)[:, i * Q : (i + 1) * Q]
    return z * f64(s) + f64(b)

@@ -1,0 +1,78 @@
+import concourse.mybir as mybir
+from concourse.masks import make_identity
+
+BF16 = mybir.dt.bfloat16
+F32 = mybir.dt.float32
+U16 = mybir.dt.uint16
+IDENTITY = mybir.ActivationFunctionType.Identity
+MULT = mybir.AluOpType.mult
+ADD = mybir.AluOpType.add
+
+P = 128
+SEQS = 2
+FEATS = 256
+TOKENS = 512
+DEPTH = 512
+LIST = 256
+PIECE = LIST // SEQS
+PIECE_COLS = PIECE // 16
+FEAT_BLOCKS = FEATS // P
+DEPTH_BLOCKS = DEPTH // P
+
+FLOPS = 2 * DEPTH * FEATS * LIST
+
+
+def tile_scatter_matmul_kernel(tc, base, x, w, s, b, offs, out):
+    nc = tc.nc
+    windows = [(i, a) for i in range(SEQS) for a in range(FEAT_BLOCKS)]
+
+    with (
+        tc.tile_pool(name="held", bufs=1) as held,
+        tc.psum_pool(name="banks", bufs=1) as banks,
+    ):
+        offsets = held.tile([P, LIST // 16], U16, name="offsets")
+        nc.sync.dma_start(offsets[:], offs)
+
+        ident = held.tile([P, P], BF16, name="ident")
+        make_identity(nc, ident[:])
+
+        base_sb = [held.tile([P, FEAT_BLOCKS, TOKENS], BF16, name="base%d" % i) for i in range(SEQS)]
+        nc.sync.dma_start(base_sb[0][:], base[0].rearrange("(a p) t -> p a t", p=P))
+        nc.scalar.dma_start(base_sb[1][:], base[1].rearrange("(a p) t -> p a t", p=P))
+
+        w_sb = held.tile([P, DEPTH_BLOCKS, FEATS], BF16, name="w_sb")
+        x_sb = held.tile([P, DEPTH_BLOCKS, LIST], BF16, name="x_sb")
+        nc.sync.dma_start(w_sb[:], w.rearrange("(p k) m -> p k m", k=DEPTH_BLOCKS))
+        nc.scalar.dma_start(x_sb[:], x.rearrange("(p k) j -> p k j", k=DEPTH_BLOCKS))
+
+        gain = held.tile([P, FEAT_BLOCKS], F32, name="gain")
+        shift = held.tile([P, FEAT_BLOCKS], F32, name="shift")
+        with nc.allow_non_contiguous_dma(reason="one float32 to a partition"):
+            nc.gpsimd.dma_start(gain[:], s.rearrange("(a p) o -> p (a o)", p=P))
+            nc.gpsimd.dma_start(shift[:], b.rearrange("(a p) o -> p (a o)", p=P))
+
+        window = {}
+        for i, a in windows:
+            window[i, a] = banks.tile([P, TOKENS], F32, name="window%d%d" % (i, a))
+            nc.tensor.matmul(window[i, a][:], ident[:], base_sb[i][:, a, :], start=True, stop=False)
+
+        for n, (i, a) in enumerate(windows):
+            piece = offsets[:, i * PIECE_COLS : (i + 1) * PIECE_COLS]
+            for k in range(DEPTH_BLOCKS):
+                nc.tensor.matmul(
+                    window[i, a][:].indirect(piece),
+                    w_sb[:, k, a * P : (a + 1) * P],
+                    x_sb[:, k, i * PIECE : (i + 1) * PIECE],
+                    start=False,
+                    stop=(k == DEPTH_BLOCKS - 1),
+                )
+            result = held.tile([P, TOKENS], F32, name="result%d%d" % (i, a))
+            if n % 2 == 0:
+                nc.vector.tensor_scalar(
+                    result[:], window[i, a][:], gain[:, a : a + 1], shift[:, a : a + 1], MULT, ADD
+                )
+            else:
+                nc.scalar.activation(
+                    result[:], window[i, a][:], IDENTITY, bias=shift[:, a : a + 1], scale=gain[:, a : a + 1]
+                )
+            nc.sync.dma_start(out[i, a * P : (a + 1) * P, :], result[:])

@@ -19,6 +19,8 @@ PIECE_COLS = PIECE // 16
 FEAT_BLOCKS = FEATS // P
 DEPTH_BLOCKS = DEPTH // P
 
+WARM_UPS = 14
+
 FLOPS = 2 * DEPTH * FEATS * LIST
 
 
@@ -30,15 +32,20 @@ def tile_scatter_matmul_kernel(tc, base, x, w, s, b, offs, out):
         tc.tile_pool(name="held", bufs=1) as held,
         tc.psum_pool(name="banks", bufs=1) as banks,
     ):
+        zeros = held.tile([P, P], BF16, name="zeros")
+        nc.vector.memset(zeros[:], 0.0)
+
         offsets = held.tile([P, LIST // 16], U16, name="offsets")
         nc.sync.dma_start(offsets[:], offs)
 
         ident = held.tile([P, P], BF16, name="ident")
         make_identity(nc, ident[:])
 
-        base_sb = [held.tile([P, FEAT_BLOCKS, TOKENS], BF16, name="base%d" % i) for i in range(SEQS)]
-        nc.sync.dma_start(base_sb[0][:], base[0].rearrange("(a p) t -> p a t", p=P))
-        nc.scalar.dma_start(base_sb[1][:], base[1].rearrange("(a p) t -> p a t", p=P))
+        base_sb = {}
+        for i, a in windows:
+            base_sb[i, a] = held.tile([P, TOKENS], BF16, name="base%d%d" % (i, a))
+            queue = nc.sync if a == 0 else nc.scalar
+            queue.dma_start(base_sb[i, a][:], base[i, a * P : (a + 1) * P, :])
 
         w_sb = held.tile([P, DEPTH_BLOCKS, FEATS], BF16, name="w_sb")
         x_sb = held.tile([P, DEPTH_BLOCKS, LIST], BF16, name="x_sb")
@@ -48,13 +55,21 @@ def tile_scatter_matmul_kernel(tc, base, x, w, s, b, offs, out):
         gain = held.tile([P, FEAT_BLOCKS], F32, name="gain")
         shift = held.tile([P, FEAT_BLOCKS], F32, name="shift")
         with nc.allow_non_contiguous_dma(reason="one float32 to a partition"):
-            nc.gpsimd.dma_start(gain[:], s.rearrange("(a p) o -> p (a o)", p=P))
-            nc.gpsimd.dma_start(shift[:], b.rearrange("(a p) o -> p (a o)", p=P))
+            nc.sync.dma_start(gain[:], s.rearrange("(a p) o -> p (a o)", p=P))
+            nc.scalar.dma_start(shift[:], b.rearrange("(a p) o -> p (a o)", p=P))
+
+        scratch = held.tile([P, 1], F32, name="scratch")
+        nc.vector.memset(scratch[:], 0.0)
+        nc.scalar.activation(scratch[:], scratch[:], IDENTITY)
+
+        spare = banks.tile([P, P], F32, name="spare")
+        for turn in range(WARM_UPS):
+            nc.tensor.matmul(spare[:], zeros[:], zeros[:], start=True, stop=True)
 
         window = {}
         for i, a in windows:
             window[i, a] = banks.tile([P, TOKENS], F32, name="window%d%d" % (i, a))
-            nc.tensor.matmul(window[i, a][:], ident[:], base_sb[i][:, a, :], start=True, stop=False)
+            nc.tensor.matmul(window[i, a][:], ident[:], base_sb[i, a][:], start=True, stop=False)
 
         for n, (i, a) in enumerate(windows):
             piece = offsets[:, i * PIECE_COLS : (i + 1) * PIECE_COLS]

@@ -82,12 +82,17 @@ def tile_scatter_matmul_kernel(tc, base, x, w, s, b, offs, out):
                     stop=(k == DEPTH_BLOCKS - 1),
                 )
             result = held.tile([P, TOKENS], F32, name="result%d%d" % (i, a))
-            if n % 2 == 0:
-                nc.vector.tensor_scalar(
-                    result[:], window[i, a][:], gain[:, a : a + 1], shift[:, a : a + 1], MULT, ADD
-                )
-            else:
-                nc.scalar.activation(
-                    result[:], window[i, a][:], IDENTITY, bias=shift[:, a : a + 1], scale=gain[:, a : a + 1]
-                )
-            nc.sync.dma_start(out[i, a * P : (a + 1) * P, :], result[:])
+            halves = 2 if n == len(windows) - 1 else 1
+            width = TOKENS // halves
+            for h in range(halves):
+                cols = slice(h * width, (h + 1) * width)
+                if n % 2 == 0:
+                    nc.vector.tensor_scalar(
+                        result[:, cols], window[i, a][:, cols], gain[:, a : a + 1], shift[:, a : a + 1], MULT, ADD
+                    )
+                else:
+                    nc.scalar.activation(
+                        result[:, cols], window[i, a][:, cols], IDENTITY,
+                        bias=shift[:, a : a + 1], scale=gain[:, a : a + 1],
+                    )
+                nc.sync.dma_start(out[i, a * P : (a + 1) * P, cols], result[:, cols])

@@ -19,8 +19,6 @@ PIECE_COLS = PIECE // 16
 FEAT_BLOCKS = FEATS // P
 DEPTH_BLOCKS = DEPTH // P
 
-WARM_UPS = 14
-
 FLOPS = 2 * DEPTH * FEATS * LIST
 
 
@@ -32,9 +30,6 @@ def tile_scatter_matmul_kernel(tc, base, x, w, s, b, offs, out):
         tc.tile_pool(name="held", bufs=1) as held,
         tc.psum_pool(name="banks", bufs=1) as banks,
     ):
-        zeros = held.tile([P, P], BF16, name="zeros")
-        nc.vector.memset(zeros[:], 0.0)
-
         offsets = held.tile([P, LIST // 16], U16, name="offsets")
         nc.sync.dma_start(offsets[:], offs)
 
@@ -61,10 +56,6 @@ def tile_scatter_matmul_kernel(tc, base, x, w, s, b, offs, out):
         scratch = held.tile([P, 1], F32, name="scratch")
         nc.vector.memset(scratch[:], 0.0)
         nc.scalar.activation(scratch[:], scratch[:], IDENTITY)
-
-        spare = banks.tile([P, P], F32, name="spare")
-        for turn in range(WARM_UPS):
-            nc.tensor.matmul(spare[:], zeros[:], zeros[:], start=True, stop=True)
 
         window = {}
         for i, a in windows:

@@ -18,6 +18,9 @@ PIECE = LIST // SEQS
 PIECE_COLS = PIECE // 16
 FEAT_BLOCKS = FEATS // P
 DEPTH_BLOCKS = DEPTH // P
+HALF_BLOCKS = DEPTH_BLOCKS // 2
+
+WARM_UPS = 14
 
 FLOPS = 2 * DEPTH * FEATS * LIST
 
@@ -30,6 +33,9 @@ def tile_scatter_matmul_kernel(tc, base, x, w, s, b, offs, out):
         tc.tile_pool(name="held", bufs=1) as held,
         tc.psum_pool(name="banks", bufs=1) as banks,
     ):
+        zeros = held.tile([P, P], BF16, name="zeros")
+        nc.vector.memset(zeros[:], 0.0)
+
         offsets = held.tile([P, LIST // 16], U16, name="offsets")
         nc.sync.dma_start(offsets[:], offs)
 
@@ -42,10 +48,15 @@ def tile_scatter_matmul_kernel(tc, base, x, w, s, b, offs, out):
             queue = nc.sync if a == 0 else nc.scalar
             queue.dma_start(base_sb[i, a][:], base[i, a * P : (a + 1) * P, :])
 
-        w_sb = held.tile([P, DEPTH_BLOCKS, FEATS], BF16, name="w_sb")
-        x_sb = held.tile([P, DEPTH_BLOCKS, LIST], BF16, name="x_sb")
-        nc.sync.dma_start(w_sb[:], w.rearrange("(p k) m -> p k m", k=DEPTH_BLOCKS))
-        nc.scalar.dma_start(x_sb[:], x.rearrange("(p k) j -> p k j", k=DEPTH_BLOCKS))
+        w_rows = w.rearrange("(p k) m -> p k m", k=DEPTH_BLOCKS)
+        x_rows = x.rearrange("(p k) j -> p k j", k=DEPTH_BLOCKS)
+        w_sb, x_sb = [], []
+        for h in range(2):
+            blocks = slice(h * HALF_BLOCKS, (h + 1) * HALF_BLOCKS)
+            w_sb.append(held.tile([P, HALF_BLOCKS, FEATS], BF16, name="w%d" % h))
+            x_sb.append(held.tile([P, HALF_BLOCKS, LIST], BF16, name="x%d" % h))
+            nc.sync.dma_start(w_sb[h][:], w_rows[:, blocks, :])
+            nc.scalar.dma_start(x_sb[h][:], x_rows[:, blocks, :])
 
         gain = held.tile([P, FEAT_BLOCKS], F32, name="gain")
         shift = held.tile([P, FEAT_BLOCKS], F32, name="shift")
@@ -57,21 +68,33 @@ def tile_scatter_matmul_kernel(tc, base, x, w, s, b, offs, out):
         nc.vector.memset(scratch[:], 0.0)
         nc.scalar.activation(scratch[:], scratch[:], IDENTITY)
 
+        spare = banks.tile([P, P], F32, name="spare")
+        for turn in range(WARM_UPS):
+            nc.tensor.matmul(spare[:], zeros[:], zeros[:], start=True, stop=True)
+
         window = {}
         for i, a in windows:
             window[i, a] = banks.tile([P, TOKENS], F32, name="window%d%d" % (i, a))
             nc.tensor.matmul(window[i, a][:], ident[:], base_sb[i, a][:], start=True, stop=False)
 
-        for n, (i, a) in enumerate(windows):
+        def scatter(i, a, h):
             piece = offsets[:, i * PIECE_COLS : (i + 1) * PIECE_COLS]
-            for k in range(DEPTH_BLOCKS):
+            for k in range(HALF_BLOCKS):
                 nc.tensor.matmul(
                     window[i, a][:].indirect(piece),
-                    w_sb[:, k, a * P : (a + 1) * P],
-                    x_sb[:, k, i * PIECE : (i + 1) * PIECE],
+                    w_sb[h][:, k, a * P : (a + 1) * P],
+                    x_sb[h][:, k, i * PIECE : (i + 1) * PIECE],
                     start=False,
-                    stop=(k == DEPTH_BLOCKS - 1),
+                    stop=(h == 1 and k == HALF_BLOCKS - 1),
                 )
+
+        for a in range(FEAT_BLOCKS):
+            scatter(0, a, 0)
+
+        for n, (i, a) in enumerate(windows):
+            if i > 0:
+                scatter(i, a, 0)
+            scatter(i, a, 1)
             result = held.tile([P, TOKENS], F32, name="result%d%d" % (i, a))
             halves = 2 if n == len(windows) - 1 else 1
             width = TOKENS // halves

@@ -36,17 +36,16 @@ def tile_scatter_matmul_kernel(tc, base, x, w, s, b, offs, out):
         zeros = held.tile([P, P], BF16, name="zeros")
         nc.vector.memset(zeros[:], 0.0)
 
-        offsets = held.tile([P, LIST // 16], U16, name="offsets")
-        nc.sync.dma_start(offsets[:], offs)
-
         ident = held.tile([P, P], BF16, name="ident")
         make_identity(nc, ident[:])
 
         base_sb = {}
         for i, a in windows:
             base_sb[i, a] = held.tile([P, TOKENS], BF16, name="base%d%d" % (i, a))
-            queue = nc.sync if a == 0 else nc.scalar
-            queue.dma_start(base_sb[i, a][:], base[i, a * P : (a + 1) * P, :])
+            nc.sync.dma_start(base_sb[i, a][:], base[i, a * P : (a + 1) * P, :])
+
+        offsets = held.tile([P, LIST // 16], U16, name="offsets")
+        nc.sync.dma_start(offsets[:], offs)
 
         w_rows = w.rearrange("(p k) m -> p k m", k=DEPTH_BLOCKS)
         x_rows = x.rearrange("(p k) j -> p k j", k=DEPTH_BLOCKS)
@@ -56,13 +55,13 @@ def tile_scatter_matmul_kernel(tc, base, x, w, s, b, offs, out):
             w_sb.append(held.tile([P, HALF_BLOCKS, FEATS], BF16, name="w%d" % h))
             x_sb.append(held.tile([P, HALF_BLOCKS, LIST], BF16, name="x%d" % h))
             nc.sync.dma_start(w_sb[h][:], w_rows[:, blocks, :])
-            nc.scalar.dma_start(x_sb[h][:], x_rows[:, blocks, :])
+            nc.sync.dma_start(x_sb[h][:], x_rows[:, blocks, :])
 
         gain = held.tile([P, FEAT_BLOCKS], F32, name="gain")
         shift = held.tile([P, FEAT_BLOCKS], F32, name="shift")
         with nc.allow_non_contiguous_dma(reason="one float32 to a partition"):
             nc.sync.dma_start(gain[:], s.rearrange("(a p) o -> p (a o)", p=P))
-            nc.scalar.dma_start(shift[:], b.rearrange("(a p) o -> p (a o)", p=P))
+            nc.sync.dma_start(shift[:], b.rearrange("(a p) o -> p (a o)", p=P))
 
         scratch = held.tile([P, 1], F32, name="scratch")
         nc.vector.memset(scratch[:], 0.0)

@@ -20,7 +20,7 @@ FEAT_BLOCKS = FEATS // P
 DEPTH_BLOCKS = DEPTH // P
 HALF_BLOCKS = DEPTH_BLOCKS // 2
 
-WARM_UPS = 14
+WARM_UPS = 9
 
 FLOPS = 2 * DEPTH * FEATS * LIST
 

@@ -40,9 +40,14 @@ def tile_scatter_matmul_kernel(tc, base, x, w, s, b, offs, out):
         make_identity(nc, ident[:])
 
         base_sb = {}
-        for i, a in windows:
-            base_sb[i, a] = held.tile([P, TOKENS], BF16, name="base%d%d" % (i, a))
-            nc.sync.dma_start(base_sb[i, a][:], base[i, a * P : (a + 1) * P, :])
+        for a in range(FEAT_BLOCKS):
+            first = held.tile([P, TOKENS], BF16, name="base0%d" % a)
+            nc.sync.dma_start(first[:], base[0, a * P : (a + 1) * P, :])
+            base_sb[0, a] = first[:]
+        second = held.tile([P, FEAT_BLOCKS, TOKENS], BF16, name="base1")
+        nc.sync.dma_start(second[:], base[1].rearrange("(a p) t -> p a t", p=P))
+        for a in range(FEAT_BLOCKS):
+            base_sb[1, a] = second[:, a, :]
 
         offsets = held.tile([P, LIST // 16], U16, name="offsets")
         nc.sync.dma_start(offsets[:], offs)
@@ -74,7 +79,7 @@ def tile_scatter_matmul_kernel(tc, base, x, w, s, b, offs, out):
         window = {}
         for i, a in windows:
             window[i, a] = banks.tile([P, TOKENS], F32, name="window%d%d" % (i, a))
-            nc.tensor.matmul(window[i, a][:], ident[:], base_sb[i, a][:], start=True, stop=False)
+            nc.tensor.matmul(window[i, a][:], ident[:], base_sb[i, a], start=True, stop=False)
 
         def scatter(i, a, h):
             piece = offsets[:, i * PIECE_COLS : (i + 1) * PIECE_COLS]
@@ -95,7 +100,7 @@ def tile_scatter_matmul_kernel(tc, base, x, w, s, b, offs, out):
                 scatter(i, a, 0)
             scatter(i, a, 1)
             result = held.tile([P, TOKENS], F32, name="result%d%d" % (i, a))
-            halves = 2 if n == len(windows) - 1 else 1
+            halves = 2 if n in (0, len(windows) - 1) else 1
             width = TOKENS // halves
             for h in range(halves):
                 cols = slice(h * width, (h + 1) * width)

@@ -39,13 +39,14 @@ def tile_scatter_matmul_kernel(tc, base, x, w, s, b, offs, out):
         ident = held.tile([P, P], BF16, name="ident")
         make_identity(nc, ident[:])
 
+        base_rows = [base[i].rearrange("(p a) t -> p a t", a=FEAT_BLOCKS) for i in range(SEQS)]
         base_sb = {}
         for a in range(FEAT_BLOCKS):
             first = held.tile([P, TOKENS], BF16, name="base0%d" % a)
-            nc.sync.dma_start(first[:], base[0, a * P : (a + 1) * P, :])
+            nc.sync.dma_start(first[:], base_rows[0][:, a, :])
             base_sb[0, a] = first[:]
         second = held.tile([P, FEAT_BLOCKS, TOKENS], BF16, name="base1")
-        nc.sync.dma_start(second[:], base[1].rearrange("(a p) t -> p a t", p=P))
+        nc.sync.dma_start(second[:], base_rows[1])
         for a in range(FEAT_BLOCKS):
             base_sb[1, a] = second[:, a, :]
 
@@ -64,9 +65,10 @@ def tile_scatter_matmul_kernel(tc, base, x, w, s, b, offs, out):
 
         gain = held.tile([P, FEAT_BLOCKS], F32, name="gain")
         shift = held.tile([P, FEAT_BLOCKS], F32, name="shift")
-        with nc.allow_non_contiguous_dma(reason="one float32 to a partition"):
-            nc.sync.dma_start(gain[:], s.rearrange("(a p) o -> p (a o)", p=P))
-            nc.sync.dma_start(shift[:], b.rearrange("(a p) o -> p (a o)", p=P))
+        nc.sync.dma_start(gain[:], s.rearrange("(p a) o -> p (a o)", a=FEAT_BLOCKS))
+        nc.sync.dma_start(shift[:], b.rearrange("(p a) o -> p (a o)", a=FEAT_BLOCKS))
+
+        out_rows = [out[i].rearrange("(p a) t -> p a t", a=FEAT_BLOCKS) for i in range(SEQS)]
 
         scratch = held.tile([P, 1], F32, name="scratch")
         nc.vector.memset(scratch[:], 0.0)
@@ -86,7 +88,7 @@ def tile_scatter_matmul_kernel(tc, base, x, w, s, b, offs, out):
             for k in range(HALF_BLOCKS):
                 nc.tensor.matmul(
                     window[i, a][:].indirect(piece),
-                    w_sb[h][:, k, a * P : (a + 1) * P],
+                    w_sb[h][:, k, a::FEAT_BLOCKS],
                     x_sb[h][:, k, i * PIECE : (i + 1) * PIECE],
                     start=False,
                     stop=(h == 1 and k == HALF_BLOCKS - 1),
@@ -113,4 +115,4 @@ def tile_scatter_matmul_kernel(tc, base, x, w, s, b, offs, out):
                         result[:, cols], window[i, a][:, cols], IDENTITY,
                         bias=shift[:, a : a + 1], scale=gain[:, a : a + 1],
                     )
-                nc.sync.dma_start(out[i, a * P : (a + 1) * P, cols], result[:, cols])
+                nc.sync.dma_start(out_rows[i][:, a, cols], result[:, cols])

import concourse.mybir as mybir
from concourse.masks import make_identity

BF16 = mybir.dt.bfloat16
F32 = mybir.dt.float32
U16 = mybir.dt.uint16
IDENTITY = mybir.ActivationFunctionType.Identity
MULT = mybir.AluOpType.mult
ADD = mybir.AluOpType.add

P = 128
SEQS = 2
FEATS = 256
TOKENS = 512
DEPTH = 512
LIST = 256
PIECE = LIST // SEQS
PIECE_COLS = PIECE // 16
FEAT_BLOCKS = FEATS // P
DEPTH_BLOCKS = DEPTH // P
HALF_BLOCKS = DEPTH_BLOCKS // 2

WARM_UPS = 9

FLOPS = 2 * DEPTH * FEATS * LIST


def tile_scatter_matmul_kernel(tc, base, x, w, s, b, offs, out):
    nc = tc.nc
    windows = [(i, a) for i in range(SEQS) for a in range(FEAT_BLOCKS)]

    with (
        tc.tile_pool(name="held", bufs=1) as held,
        tc.psum_pool(name="banks", bufs=1) as banks,
    ):
        zeros = held.tile([P, P], BF16, name="zeros")
        nc.vector.memset(zeros[:], 0.0)

        ident = held.tile([P, P], BF16, name="ident")
        make_identity(nc, ident[:])

        base_rows = [base[i].rearrange("(p a) t -> p a t", a=FEAT_BLOCKS) for i in range(SEQS)]
        base_sb = {}
        for a in range(FEAT_BLOCKS):
            first = held.tile([P, TOKENS], BF16, name="base0%d" % a)
            nc.sync.dma_start(first[:], base_rows[0][:, a, :])
            base_sb[0, a] = first[:]
        second = held.tile([P, FEAT_BLOCKS, TOKENS], BF16, name="base1")
        nc.sync.dma_start(second[:], base_rows[1])
        for a in range(FEAT_BLOCKS):
            base_sb[1, a] = second[:, a, :]

        offsets = held.tile([P, LIST // 16], U16, name="offsets")
        nc.sync.dma_start(offsets[:], offs)

        w_rows = w.rearrange("(p k) m -> p k m", k=DEPTH_BLOCKS)
        x_rows = x.rearrange("(p k) j -> p k j", k=DEPTH_BLOCKS)
        w_sb, x_sb = [], []
        for h in range(2):
            blocks = slice(h * HALF_BLOCKS, (h + 1) * HALF_BLOCKS)
            w_sb.append(held.tile([P, HALF_BLOCKS, FEATS], BF16, name="w%d" % h))
            x_sb.append(held.tile([P, HALF_BLOCKS, LIST], BF16, name="x%d" % h))
            nc.sync.dma_start(w_sb[h][:], w_rows[:, blocks, :])
            nc.sync.dma_start(x_sb[h][:], x_rows[:, blocks, :])

        gain = held.tile([P, FEAT_BLOCKS], F32, name="gain")
        shift = held.tile([P, FEAT_BLOCKS], F32, name="shift")
        nc.sync.dma_start(gain[:], s.rearrange("(p a) o -> p (a o)", a=FEAT_BLOCKS))
        nc.sync.dma_start(shift[:], b.rearrange("(p a) o -> p (a o)", a=FEAT_BLOCKS))

        out_rows = [out[i].rearrange("(p a) t -> p a t", a=FEAT_BLOCKS) for i in range(SEQS)]

        scratch = held.tile([P, 1], F32, name="scratch")
        nc.vector.memset(scratch[:], 0.0)
        nc.scalar.activation(scratch[:], scratch[:], IDENTITY)

        spare = banks.tile([P, P], F32, name="spare")
        for turn in range(WARM_UPS):
            nc.tensor.matmul(spare[:], zeros[:], zeros[:], start=True, stop=True)

        window = {}
        for i, a in windows:
            window[i, a] = banks.tile([P, TOKENS], F32, name="window%d%d" % (i, a))
            nc.tensor.matmul(window[i, a][:], ident[:], base_sb[i, a], start=True, stop=False)

        def scatter(i, a, h):
            piece = offsets[:, i * PIECE_COLS : (i + 1) * PIECE_COLS]
            for k in range(HALF_BLOCKS):
                nc.tensor.matmul(
                    window[i, a][:].indirect(piece),
                    w_sb[h][:, k, a::FEAT_BLOCKS],
                    x_sb[h][:, k, i * PIECE : (i + 1) * PIECE],
                    start=False,
                    stop=(h == 1 and k == HALF_BLOCKS - 1),
                )

        for a in range(FEAT_BLOCKS):
            scatter(0, a, 0)

        for n, (i, a) in enumerate(windows):
            if i > 0:
                scatter(i, a, 0)
            scatter(i, a, 1)
            result = held.tile([P, TOKENS], F32, name="result%d%d" % (i, a))
            halves = 2 if n in (0, len(windows) - 1) else 1
            width = TOKENS // halves
            for h in range(halves):
                cols = slice(h * width, (h + 1) * width)
                if n % 2 == 0:
                    nc.vector.tensor_scalar(
                        result[:, cols], window[i, a][:, cols], gain[:, a : a + 1], shift[:, a : a + 1], MULT, ADD
                    )
                else:
                    nc.scalar.activation(
                        result[:, cols], window[i, a][:, cols], IDENTITY,
                        bias=shift[:, a : a + 1], scale=gain[:, a : a + 1],
                    )
                nc.sync.dma_start(out_rows[i][:, a, cols], result[:, cols])
